import numpy as np
import ml_dtypes


def mxq(x, axis, fmt="e4m3"):
    dtype, down = {"e4m3": (ml_dtypes.float8_e4m3fn, 7), "e5m2": (ml_dtypes.float8_e5m2, 14)}[fmt]
    v = np.moveaxis(np.asarray(x, np.float32).astype(ml_dtypes.bfloat16).astype(np.float64), axis, -1)
    blocks = v.reshape(v.shape[:-1] + (-1, 32))
    amax = np.abs(blocks).max(-1, keepdims=True)
    byte = np.maximum(np.where(amax > 0, np.frexp(amax)[1] - 1 + 127, 0) - down, 1)
    scale = np.exp2(byte - 127.0)
    codes = (blocks / scale).astype(np.float32).astype(dtype).astype(np.float64)
    return np.moveaxis((codes * scale).reshape(v.shape), -1, axis)


WIDE = False


def mx_kscale(k):
    if not WIDE:
        return np.ones(k)
    levels = np.array([10, -10, 5, -5, 0])
    if k % 512:
        return np.exp2(np.random.permutation(np.resize(levels, k // 32))).repeat(32)
    a = np.empty((k // 512, 16))
    for p in range(k // 512):
        a[p, :8] = np.random.permutation(np.resize(levels, 8))
        for g in range(8):
            far = levels[np.abs(levels - a[p, g]) >= 10]
            a[p, g + 8] = far[np.random.randint(len(far))]
    return np.exp2(a.ravel()).repeat(32)


def f64(x):
    return np.asarray(x).astype(np.float64)


def striped(idx):
    return np.tile(idx.reshape(-1, 16).T, (8, 1)).astype(np.uint16)


def unstriped(offs):
    return offs[:16].T.reshape(-1).astype(np.int64)


def relu(v):
    return np.maximum(v, 0.0)


K, T, S, H, N = 1024, 1024, 512, 512, 128


def setup_inputs():
    n = np.random.standard_normal
    s = mx_kscale(K)[:, None]
    u = mx_kscale(H)
    return {
        "xT": (n((K, T)) * s).astype(np.float32),
        "w1": (n((K, N)) / np.sqrt(2 * K) / s).astype(np.float32),
        "w2": (n((K, H)) / np.sqrt(K) / s * u).astype(np.float32),
        "w3": (n((H, N)) / np.sqrt(2 * H) / u[:, None]).astype(np.float32),
        "offs": striped(np.random.permutation(T)[:S]),
    }


def reference(xT, w1, w2, w3, offs):
    xq = mxq(f64(xT)[:, unstriped(offs)], 0, "e4m3")
    h = relu(mxq(f64(w2), 0, "e4m3").T @ xq)
    return mxq(f64(w1), 0, "e4m3").T @ xq + mxq(f64(w3), 0, "e4m3").T @ mxq(h, 0, "e4m3")

@@ -1,0 +1,256 @@
+from contextlib import ExitStack
+
+import concourse.mybir as mybir
+
+K, T, S, H, N = 1024, 1024, 512, 512, 128
+FLOPS = 2 * S * (K * N + K * H + H * N)
+
+F32 = mybir.dt.float32
+BF16 = mybir.dt.bfloat16
+U32 = mybir.dt.uint32
+U16 = mybir.dt.uint16
+U8 = mybir.dt.uint8
+FP8X4 = mybir.dt.float8_e4m3fn_x4
+COPY = mybir.ActivationFunctionType.Copy
+RELU = mybir.ActivationFunctionType.Relu
+MAX = mybir.AluOpType.max
+
+P = 128
+PACK = 4
+K_PASS = P * PACK
+CHUNK = 128
+CHUNKS = S // CHUNK
+X_PIECES = ((0, 0, 512), (0, 512, 512), (1, 0, 512), (1, 512, 256), (1, 768, 256))
+W2_PIECES = ((0, 0, 256), (0, 256, 256), (1, 0, 256), (1, 256, 256))
+
+
+def tile_picked_lora_relu_e_kernel(tc, xT, w1, w2, w3, offs, out):
+    nc = tc.nc
+    with ExitStack() as ctx:
+        keep = ctx.enter_context(tc.tile_pool(name="keep", bufs=1))
+        psum = ctx.enter_context(tc.psum_pool(name="psum", bufs=1))
+
+        def sb(name, shape, dtype):
+            return keep.tile(shape, dtype, name=name, align_bytes=64)
+
+        offsets = keep.tile([P, S // 16], U16, name="offsets")
+        x_scales = [sb("x_scales%d" % z, [P, T], U8) for z in range(2)]
+        for z in range(2):
+            nc.gpsimd.memset(x_scales[z][:].bitcast(U32), 0)
+
+        x_raw = {}
+        w2_raw = {}
+        w1_raw = sb("w1_raw", [P, 2, PACK, N], F32)
+        w3_raw = sb("w3_raw", [P, PACK, N], F32)
+
+        def load_x(n):
+            z, c0, width = X_PIECES[n]
+            x_raw[n] = sb("x_raw%d" % n, [P, PACK, width], F32)
+            rows = xT[z * K_PASS : (z + 1) * K_PASS, c0 : c0 + width]
+            nc.sync.dma_start(out=x_raw[n][:], in_=rows.rearrange("(p j) w -> p j w", j=PACK))
+
+        def load_w2(n):
+            z, c0, width = W2_PIECES[n]
+            w2_raw[n] = sb("w2_raw%d" % n, [P, PACK, width], F32)
+            rows = w2[z * K_PASS : (z + 1) * K_PASS, c0 : c0 + width]
+            nc.sync.dma_start(out=w2_raw[n][:], in_=rows.rearrange("(p j) w -> p j w", j=PACK))
+
+        def load_offs():
+            nc.sync.dma_start(offsets[:], offs)
+
+        def load_w1():
+            nc.sync.dma_start(out=w1_raw[:], in_=w1.rearrange("(z p j) n -> p z j n", z=2, j=PACK))
+
+        def load_w3():
+            w3_rows = w3.rearrange("(g t r) n -> t g r n", t=PACK, r=8)
+            for t in range(PACK):
+                nc.sync.dma_start(out=w3_raw[:, t, :], in_=w3_rows[t])
+
+        def weave(engine, dst, src):
+            dst = dst.rearrange("p (c i) j -> p c j i", i=4)
+            src = src.rearrange("p j (c i) -> p c j i", i=4)
+            if engine == "S":
+                nc.scalar.activation(dst, src, COPY)
+            else:
+                nc.vector.tensor_copy(dst, src)
+
+        def quantize(codes, scales, values):
+            nc.vector.quantize_mx(out=codes.bitcast(FP8X4), scales=scales, in_=values)
+
+        x_codes = [sb("x_codes%d" % z, [P, T], U32) for z in range(2)]
+        picked_codes = [sb("picked_codes%d" % z, [P, S], U32) for z in range(2)]
+        picked_scales = [sb("picked_scales%d" % z, [P, S], U8) for z in range(2)]
+        x_bf = [sb("x_bf%d" % n, [P, X_PIECES[n][2], PACK], BF16) for n in range(len(X_PIECES))]
+
+        def weave_x(n, engine, a, b):
+            weave(engine, x_bf[n][:, a:b, :], x_raw[n][:, :, a:b])
+
+        def quant_x(n):
+            z, c0, width = X_PIECES[n]
+            quantize(x_codes[z][:, c0 : c0 + width], x_scales[z][:, c0 : c0 + width], x_bf[n][:].rearrange("p w j -> p (w j)"))
+
+        def pick_codes(z):
+            nc.vector.tensor_copy(picked_codes[z][:], x_codes[z][:].indirect(offsets[:]))
+
+        def pick_scales(z):
+            nc.vector.tensor_copy(picked_scales[z][:], x_scales[z][:].indirect(offsets[:]))
+
+        h_acc = [psum.tile([P, PACK, CHUNK], F32, name="h_acc%d" % c) for c in range(CHUNKS)]
+        out_acc = [psum.tile([P, S], F32, name="out_acc%d" % c) for c in range(CHUNKS)]
+        w2_bf = [sb("w2_bf%d" % z, [P, PACK, P, PACK], BF16) for z in range(2)]
+        w2_codes = [sb("w2_codes%d" % z, [P, H], U32) for z in range(2)]
+        w2_scales = [sb("w2_scales%d" % z, [P, H], U8) for z in range(2)]
+
+        def weave_w2(n, engine, t, g0=0, g1=None):
+            z, c0, width = W2_PIECES[n]
+            g1 = width // 32 if g1 is None else g1
+            m0 = c0 // PACK
+            src = w2_raw[n][:, :, 32 * g0 : 32 * g1].rearrange("p j (g t a i) -> p t g a j i", t=PACK, a=2, i=4)
+            dst = w2_bf[z][:, t, m0 + 8 * g0 : m0 + 8 * g1, :].rearrange("p (g a i) j -> p g a j i", a=2, i=4)
+            if engine == "S":
+                nc.scalar.copy(dst, src[:, t])
+            else:
+                nc.vector.tensor_copy(dst, src[:, t])
+
+        def quant_w2(z, t0=0, t1=PACK):
+            quantize(w2_codes[z][:, t0 * P : t1 * P], w2_scales[z][:, t0 * P : t1 * P], w2_bf[z][:, t0:t1].rearrange("p t w j -> p (t w j)"))
+
+        def h_pass(z, t, c):
+            cols = slice(c * CHUNK, (c + 1) * CHUNK)
+            nc.tensor.matmul_mx(
+                out=h_acc[c][:, t, :],
+                lhsT=w2_codes[z][:, t * P : (t + 1) * P].bitcast(FP8X4),
+                lhsT_scale=w2_scales[z][:, t * P : (t + 1) * P],
+                rhs=picked_codes[z][:, cols].bitcast(FP8X4),
+                rhs_scale=picked_scales[z][:, cols],
+                start=(z == 0 and t == 0),
+                stop=(z == 1 and t == PACK - 1),
+            )
+
+        def warm(z, width):
+            nc.tensor.matmul_mx(
+                out=out_acc[CHUNKS - 1][:, :width],
+                lhsT=picked_codes[0][:, :P].bitcast(FP8X4),
+                lhsT_scale=picked_scales[0][:, :P],
+                rhs=picked_codes[z][:, :width].bitcast(FP8X4),
+                rhs_scale=picked_scales[0][:, :width],
+                start=True,
+                stop=True,
+            )
+
+        w1_bf = sb("w1_bf", [P, 2, N, PACK], BF16)
+        w1_codes = sb("w1_codes", [P, 2 * N], U32)
+        w1_scales = sb("w1_scales", [P, 2 * N], U8)
+        w3_bf = sb("w3_bf", [P, N, PACK], BF16)
+        w3_codes = sb("w3_codes", [P, N], U32)
+        w3_scales = sb("w3_scales", [P, N], U8)
+        h_bf = [sb("h_bf%d" % c, [P, CHUNK, PACK], BF16) for c in range(CHUNKS)]
+        h_codes = [sb("h_codes%d" % c, [P, CHUNK], U32) for c in range(CHUNKS)]
+        h_scales = [sb("h_scales%d" % c, [P, CHUNK], U8) for c in range(CHUNKS)]
+
+        def weave_w1(z, engine):
+            weave(engine, w1_bf[:, z], w1_raw[:, z])
+
+        def weave_w3(engine):
+            weave(engine, w3_bf[:], w3_raw[:])
+
+        def quant_w1():
+            quantize(w1_codes[:], w1_scales[:], w1_bf[:].rearrange("p z w j -> p (z w j)"))
+
+        def quant_w3():
+            quantize(w3_codes[:], w3_scales[:], w3_bf[:].rearrange("p w j -> p (w j)"))
+
+        def relu(c, engine):
+            src = h_acc[c][:].rearrange("p t n -> p n t")
+            if engine == "S":
+                nc.scalar.activation(h_bf[c][:], src, RELU)
+            else:
+                nc.vector.tensor_scalar(h_bf[c][:], src, 0.0, None, MAX)
+
+        def quant_h(c):
+            quantize(h_codes[c][:], h_scales[c][:], h_bf[c][:].rearrange("p w j -> p (w j)"))
+
+        def out_pass(c, n):
+            cols = slice(c * CHUNK, (c + 1) * CHUNK)
+            if n < 2:
+                lhs, lhs_scale = w1_codes[:, n * N : (n + 1) * N], w1_scales[:, n * N : (n + 1) * N]
+                rhs, rhs_scale = picked_codes[n][:, cols], picked_scales[n][:, cols]
+            else:
+                lhs, lhs_scale = w3_codes[:], w3_scales[:]
+                rhs, rhs_scale = h_codes[c][:], h_scales[c][:]
+            nc.tensor.matmul_mx(
+                out=out_acc[c][:, :CHUNK], lhsT=lhs.bitcast(FP8X4), lhsT_scale=lhs_scale,
+                rhs=rhs.bitcast(FP8X4), rhs_scale=rhs_scale, start=(n == 0), stop=(n == 2),
+            )
+
+        def finish(c, engine):
+            result = sb("result%d" % c, [P, CHUNK], F32)
+            if engine == "S":
+                nc.scalar.copy(result[:], out_acc[c][:, :CHUNK])
+            else:
+                nc.vector.tensor_copy(result[:], out_acc[c][:, :CHUNK])
+            nc.sync.dma_start(out=out[:, c * CHUNK : (c + 1) * CHUNK], in_=result[:])
+
+        load_x(0)
+        load_offs()
+        for n in range(1, 5):
+            load_x(n)
+        for n in range(4):
+            load_w2(n)
+        load_w1()
+        load_w3()
+        weave_x(0, "S", 0, 256)
+        weave_x(0, "V", 256, 512)
+        quant_x(0)
+        weave_x(1, "S", 0, 256)
+        weave_x(1, "V", 256, 512)
+        quant_x(1)
+        pick_codes(0)
+        weave_x(2, "S", 0, 512)
+        pick_scales(0)
+        quant_x(2)
+        weave_x(3, "S", 0, 128)
+        weave_x(3, "V", 128, 256)
+        weave_x(4, "S", 0, 96)
+        quant_x(3)
+        weave_x(4, "V", 96, 256)
+        quant_x(4)
+        pick_codes(1)
+        for t in range(4):
+            weave_w2(0, "S", t)
+        weave_w2(1, "S", 0)
+        for t in range(1, 4):
+            weave_w2(1, "V", t)
+        quant_w2(0)
+        for t in range(4):
+            for c in range(CHUNKS):
+                h_pass(0, t, c)
+        for t in range(4):
+            weave_w2(2, "S", t)
+        pick_scales(1)
+        weave_w2(3, "S", 0)
+        for t in range(1, 4):
+            weave_w2(3, "V", t)
+        quant_w2(1)
+        for c in range(CHUNKS):
+            for t in range(4):
+                h_pass(1, t, c)
+        weave_w1(0, "S")
+        weave_w1(1, "V")
+        weave_w3("V")
+        relu(0, "S")
+        quant_w1()
+        quant_w3()
+        relu(1, "S")
+        for n in range(2):
+            for c in range(CHUNKS):
+                out_pass(c, n)
+        quant_h(0)
+        relu(2, "S")
+        relu(3, "V")
+        for c in range(1, CHUNKS):
+            quant_h(c)
+        for c in range(CHUNKS):
+            out_pass(c, 2)
+        for c in range(CHUNKS):
+            finish(c, "S")

@@ -20,7 +20,9 @@ PACK = 4
 K_PASS = P * PACK
 CHUNK = 128
 CHUNKS = S // CHUNK
-X_PIECES = ((0, 0, 512), (0, 512, 512), (1, 0, 512), (1, 512, 256), (1, 768, 256))
+X_PIECES = ((0, 0, 256), (0, 256, 256), (0, 512, 512), (1, 0, 256), (1, 256, 512), (1, 768, 256))
+TAGS = {"h_codes0":"w3_raw","h_codes1":"w1_raw","w3_bf":"w2_bf1_3"}
+FIRST = ((0, 0, 0, 0), (0, 0, 0, 0))
 W2_PIECES = ((0, 0, 256), (0, 256, 256), (1, 0, 256), (1, 256, 256))
 
 
@@ -30,13 +32,16 @@ def tile_picked_lora_relu_e_kernel(tc, xT, w1, w2, w3, offs, out):
         keep = ctx.enter_context(tc.tile_pool(name="keep", bufs=1))
         psum = ctx.enter_context(tc.psum_pool(name="psum", bufs=1))
 
-        def sb(name, shape, dtype):
-            return keep.tile(shape, dtype, name=name, align_bytes=64)
+        made = {}
+
+        def sb(name, shape=None, dtype=None):
+            if name not in made:
+                made[name] = keep.tile(shape, dtype, name=name, tag=TAGS.get(name, name), align_bytes=64)
+            return made[name]
 
         offsets = keep.tile([P, S // 16], U16, name="offsets")
-        x_scales = [sb("x_scales%d" % z, [P, T], U8) for z in range(2)]
-        for z in range(2):
-            nc.gpsimd.memset(x_scales[z][:].bitcast(U32), 0)
+        x_planes = sb("x_planes", [P, T], U8)
+        nc.gpsimd.memset(x_planes[:].bitcast(U32), 0)
 
         x_raw = {}
         w2_raw = {}
@@ -61,10 +66,9 @@ def tile_picked_lora_relu_e_kernel(tc, xT, w1, w2, w3, offs, out):
         def load_w1():
             nc.sync.dma_start(out=w1_raw[:], in_=w1.rearrange("(z p j) n -> p z j n", z=2, j=PACK))
 
-        def load_w3():
+        def load_w3(t):
             w3_rows = w3.rearrange("(g t r) n -> t g r n", t=PACK, r=8)
-            for t in range(PACK):
-                nc.sync.dma_start(out=w3_raw[:, t, :], in_=w3_rows[t])
+            nc.sync.dma_start(out=w3_raw[:, t, :], in_=w3_rows[t])
 
         def weave(engine, dst, src):
             dst = dst.rearrange("p (c i) j -> p c j i", i=4)
@@ -78,8 +82,6 @@ def tile_picked_lora_relu_e_kernel(tc, xT, w1, w2, w3, offs, out):
             nc.vector.quantize_mx(out=codes.bitcast(FP8X4), scales=scales, in_=values)
 
         x_codes = [sb("x_codes%d" % z, [P, T], U32) for z in range(2)]
-        picked_codes = [sb("picked_codes%d" % z, [P, S], U32) for z in range(2)]
-        picked_scales = [sb("picked_scales%d" % z, [P, S], U8) for z in range(2)]
         x_bf = [sb("x_bf%d" % n, [P, X_PIECES[n][2], PACK], BF16) for n in range(len(X_PIECES))]
 
         def weave_x(n, engine, a, b):
@@ -87,17 +89,26 @@ def tile_picked_lora_relu_e_kernel(tc, xT, w1, w2, w3, offs, out):
 
         def quant_x(n):
             z, c0, width = X_PIECES[n]
-            quantize(x_codes[z][:, c0 : c0 + width], x_scales[z][:, c0 : c0 + width], x_bf[n][:].rearrange("p w j -> p (w j)"))
+            quantize(x_codes[z][:, c0 : c0 + width], x_planes[4 * z :, c0 : c0 + width], x_bf[n][:].rearrange("p w j -> p (w j)"))
 
-        def pick_codes(z):
-            nc.vector.tensor_copy(picked_codes[z][:], x_codes[z][:].indirect(offsets[:]))
+        def pick_codes(z, a, b):
+            nc.vector.tensor_copy(sb("pc%d_%d" % (z, a), [P, (b - a) * CHUNK], U32)[:], x_codes[z][:].indirect(offsets[:, 8 * a : 8 * b]))
 
-        def pick_scales(z):
-            nc.vector.tensor_copy(picked_scales[z][:], x_scales[z][:].indirect(offsets[:]))
+        def pick_scales(z, a, b):
+            nc.vector.tensor_copy(sb("ps%d_%d" % (z, a), [P, (b - a) * CHUNK], U8)[:], x_planes[:].indirect(offsets[:, 8 * a : 8 * b]))
+
+        def picked(z, c, width=CHUNK):
+            a = FIRST[z][c]
+            codes = sb("pc%d_%d" % (z, a))[:, (c - a) * CHUNK : (c - a) * CHUNK + width]
+            a = FIRST[1][c]
+            return codes.bitcast(FP8X4), sb("ps1_%d" % a)[4 * z :, (c - a) * CHUNK : (c - a) * CHUNK + width]
+
+        def probe(name, src):
+            clock = sb(name, [P, 1], BF16)
+            nc.gpsimd.tensor_copy(clock[:], src)
 
         h_acc = [psum.tile([P, PACK, CHUNK], F32, name="h_acc%d" % c) for c in range(CHUNKS)]
         out_acc = [psum.tile([P, S], F32, name="out_acc%d" % c) for c in range(CHUNKS)]
-        w2_bf = [sb("w2_bf%d" % z, [P, PACK, P, PACK], BF16) for z in range(2)]
         w2_codes = [sb("w2_codes%d" % z, [P, H], U32) for z in range(2)]
         w2_scales = [sb("w2_scales%d" % z, [P, H], U8) for z in range(2)]
 
@@ -106,14 +117,14 @@ def tile_picked_lora_relu_e_kernel(tc, xT, w1, w2, w3, offs, out):
             g1 = width // 32 if g1 is None else g1
             m0 = c0 // PACK
             src = w2_raw[n][:, :, 32 * g0 : 32 * g1].rearrange("p j (g t a i) -> p t g a j i", t=PACK, a=2, i=4)
-            dst = w2_bf[z][:, t, m0 + 8 * g0 : m0 + 8 * g1, :].rearrange("p (g a i) j -> p g a j i", a=2, i=4)
+            dst = sb("w2_bf%d_%d" % (z, t), [P, P, PACK], BF16)[:, m0 + 8 * g0 : m0 + 8 * g1, :].rearrange("p (g a i) j -> p g a j i", a=2, i=4)
             if engine == "S":
                 nc.scalar.copy(dst, src[:, t])
             else:
                 nc.vector.tensor_copy(dst, src[:, t])
 
         def quant_w2(z, t0=0, t1=PACK):
-            quantize(w2_codes[z][:, t0 * P : t1 * P], w2_scales[z][:, t0 * P : t1 * P], w2_bf[z][:, t0:t1].rearrange("p t w j -> p (t w j)"))
+            quantize(w2_codes[z][:, t0 * P : t1 * P], w2_scales[z][:, t0 * P : t1 * P], sb("w2_bf%d_%d" % (z, t0))[:].rearrange("p w j -> p (w j)"))
 
         def h_pass(z, t, c):
             cols = slice(c * CHUNK, (c + 1) * CHUNK)
@@ -121,8 +132,8 @@ def tile_picked_lora_relu_e_kernel(tc, xT, w1, w2, w3, offs, out):
                 out=h_acc[c][:, t, :],
                 lhsT=w2_codes[z][:, t * P : (t + 1) * P].bitcast(FP8X4),
                 lhsT_scale=w2_scales[z][:, t * P : (t + 1) * P],
-                rhs=picked_codes[z][:, cols].bitcast(FP8X4),
-                rhs_scale=picked_scales[z][:, cols],
+                rhs=picked(z, c)[0],
+                rhs_scale=picked(z, c)[1],
                 start=(z == 0 and t == 0),
                 stop=(z == 1 and t == PACK - 1),
             )
@@ -130,57 +141,54 @@ def tile_picked_lora_relu_e_kernel(tc, xT, w1, w2, w3, offs, out):
         def warm(z, width):
             nc.tensor.matmul_mx(
                 out=out_acc[CHUNKS - 1][:, :width],
-                lhsT=picked_codes[0][:, :P].bitcast(FP8X4),
-                lhsT_scale=picked_scales[0][:, :P],
-                rhs=picked_codes[z][:, :width].bitcast(FP8X4),
-                rhs_scale=picked_scales[0][:, :width],
+                lhsT=picked(0, 0)[0],
+                lhsT_scale=picked(0, 0)[1],
+                rhs=picked(z, 0, width)[0],
+                rhs_scale=picked(0, 0, width)[1],
                 start=True,
                 stop=True,
             )
 
-        w1_bf = sb("w1_bf", [P, 2, N, PACK], BF16)
         w1_codes = sb("w1_codes", [P, 2 * N], U32)
         w1_scales = sb("w1_scales", [P, 2 * N], U8)
-        w3_bf = sb("w3_bf", [P, N, PACK], BF16)
         w3_codes = sb("w3_codes", [P, N], U32)
         w3_scales = sb("w3_scales", [P, N], U8)
-        h_bf = [sb("h_bf%d" % c, [P, CHUNK, PACK], BF16) for c in range(CHUNKS)]
-        h_codes = [sb("h_codes%d" % c, [P, CHUNK], U32) for c in range(CHUNKS)]
         h_scales = [sb("h_scales%d" % c, [P, CHUNK], U8) for c in range(CHUNKS)]
 
         def weave_w1(z, engine):
-            weave(engine, w1_bf[:, z], w1_raw[:, z])
+            weave(engine, sb("w1_bf", [P, 2, N, PACK], BF16)[:, z], w1_raw[:, z])
 
         def weave_w3(engine):
-            weave(engine, w3_bf[:], w3_raw[:])
+            weave(engine, sb("w3_bf", [P, N, PACK], BF16)[:], w3_raw[:])
 
         def quant_w1():
-            quantize(w1_codes[:], w1_scales[:], w1_bf[:].rearrange("p z w j -> p (z w j)"))
+            quantize(w1_codes[:], w1_scales[:], sb("w1_bf")[:].rearrange("p z w j -> p (z w j)"))
 
         def quant_w3():
-            quantize(w3_codes[:], w3_scales[:], w3_bf[:].rearrange("p w j -> p (w j)"))
+            quantize(w3_codes[:], w3_scales[:], sb("w3_bf")[:].rearrange("p w j -> p (w j)"))
 
         def relu(c, engine):
             src = h_acc[c][:].rearrange("p t n -> p n t")
+            dst = sb("h_bf%d" % c, [P, CHUNK, PACK], BF16)
             if engine == "S":
-                nc.scalar.activation(h_bf[c][:], src, RELU)
+                nc.scalar.activation(dst[:], src, RELU)
             else:
-                nc.vector.tensor_scalar(h_bf[c][:], src, 0.0, None, MAX)
+                nc.vector.tensor_scalar(dst[:], src, 0.0, None, MAX)
 
         def quant_h(c):
-            quantize(h_codes[c][:], h_scales[c][:], h_bf[c][:].rearrange("p w j -> p (w j)"))
+            quantize(sb("h_codes%d" % c, [P, CHUNK], U32)[:], h_scales[c][:], sb("h_bf%d" % c)[:].rearrange("p w j -> p (w j)"))
 
         def out_pass(c, n):
             cols = slice(c * CHUNK, (c + 1) * CHUNK)
             if n < 2:
                 lhs, lhs_scale = w1_codes[:, n * N : (n + 1) * N], w1_scales[:, n * N : (n + 1) * N]
-                rhs, rhs_scale = picked_codes[n][:, cols], picked_scales[n][:, cols]
+                rhs, rhs_scale = picked(n, c)
             else:
                 lhs, lhs_scale = w3_codes[:], w3_scales[:]
-                rhs, rhs_scale = h_codes[c][:], h_scales[c][:]
+                rhs, rhs_scale = sb("h_codes%d" % c)[:].bitcast(FP8X4), h_scales[c][:]
             nc.tensor.matmul_mx(
                 out=out_acc[c][:, :CHUNK], lhsT=lhs.bitcast(FP8X4), lhsT_scale=lhs_scale,
-                rhs=rhs.bitcast(FP8X4), rhs_scale=rhs_scale, start=(n == 0), stop=(n == 2),
+                rhs=rhs, rhs_scale=rhs_scale, start=(n == 0), stop=(n == 2),
             )
 
         def finish(c, engine):
@@ -193,64 +201,126 @@ def tile_picked_lora_relu_e_kernel(tc, xT, w1, w2, w3, offs, out):
 
         load_x(0)
         load_offs()
-        for n in range(1, 5):
-            load_x(n)
-        for n in range(4):
-            load_w2(n)
+        load_x(1)
+        load_x(2)
+        load_x(3)
+        load_x(4)
+        load_x(5)
+        load_w2(0)
+        load_w2(1)
+        load_w2(2)
+        load_w3(0)
+        load_w3(1)
+        load_w3(2)
+        load_w3(3)
+        load_w2(3)
         load_w1()
-        load_w3()
         weave_x(0, "S", 0, 256)
-        weave_x(0, "V", 256, 512)
+        weave_x(1, "S", 0, 224)
         quant_x(0)
-        weave_x(1, "S", 0, 256)
-        weave_x(1, "V", 256, 512)
+        weave_x(1, "V", 224, 256)
         quant_x(1)
-        pick_codes(0)
-        weave_x(2, "S", 0, 512)
-        pick_scales(0)
+        weave_x(2, "S", 0, 160)
+        weave_x(2, "V", 160, 512)
+        weave_x(3, "S", 0, 208)
+        weave_x(3, "V", 208, 256)
         quant_x(2)
-        weave_x(3, "S", 0, 128)
-        weave_x(3, "V", 128, 256)
-        weave_x(4, "S", 0, 96)
+        pick_codes(0, 0, 4)
+        weave_x(4, "S", 0, 224)
         quant_x(3)
-        weave_x(4, "V", 96, 256)
+        weave_x(4, "V", 224, 512)
+        weave_x(5, "S", 0, 208)
+        weave_w2(0, "S", 0, 0, 6)
+        weave_x(5, "V", 208, 256)
         quant_x(4)
-        pick_codes(1)
-        for t in range(4):
-            weave_w2(0, "S", t)
-        weave_w2(1, "S", 0)
-        for t in range(1, 4):
-            weave_w2(1, "V", t)
-        quant_w2(0)
-        for t in range(4):
-            for c in range(CHUNKS):
-                h_pass(0, t, c)
-        for t in range(4):
-            weave_w2(2, "S", t)
-        pick_scales(1)
-        weave_w2(3, "S", 0)
-        for t in range(1, 4):
-            weave_w2(3, "V", t)
-        quant_w2(1)
-        for c in range(CHUNKS):
-            for t in range(4):
-                h_pass(1, t, c)
-        weave_w1(0, "S")
+        weave_w2(0, "S", 2, 0, 8)
+        quant_x(5)
+        weave_w2(0, "V", 0, 6, 8)
+        weave_w2(0, "S", 3, 0, 8)
+        pick_scales(1, 0, 4)
+        weave_w2(0, "S", 1, 0, 8)
+        weave_w2(1, "S", 1, 0, 8)
+        weave_w2(2, "S", 3, 0, 8)
+        weave_w2(1, "S", 0, 0, 8)
+        weave_w2(1, "S", 3, 0, 8)
+        pick_codes(1, 0, 4)
+        weave_w2(1, "S", 2, 0, 8)
+        weave_w2(2, "S", 1, 0, 8)
+        warm(0, 512)
+        warm(0, 512)
+        quant_w2(0, 3, 4)
+        weave_w2(2, "S", 0, 0, 8)
+        quant_w2(0, 1, 2)
+        warm(0, 256)
+        quant_w2(0, 0, 1)
+        h_pass(0, 0, 1)
+        weave_w2(2, "S", 2, 0, 8)
+        quant_w2(0, 2, 3)
+        h_pass(0, 0, 0)
+        h_pass(0, 0, 3)
+        h_pass(0, 0, 2)
+        h_pass(0, 1, 3)
+        weave_w2(3, "S", 3, 0, 8)
+        weave_w2(3, "V", 0, 0, 8)
+        h_pass(0, 1, 0)
+        h_pass(0, 1, 2)
+        h_pass(0, 1, 1)
+        weave_w2(3, "V", 1, 0, 8)
+        h_pass(0, 2, 3)
+        weave_w2(3, "S", 2, 0, 8)
+        h_pass(0, 2, 0)
+        h_pass(0, 2, 2)
+        quant_w2(1, 0, 1)
+        h_pass(0, 3, 0)
+        h_pass(0, 3, 3)
+        quant_w2(1, 1, 2)
+        h_pass(0, 3, 2)
+        h_pass(0, 2, 1)
+        h_pass(0, 3, 1)
+        quant_w2(1, 3, 4)
+        h_pass(1, 0, 1)
+        quant_w2(1, 2, 3)
+        h_pass(1, 0, 0)
+        h_pass(1, 0, 2)
+        weave_w1(0, "V")
+        weave_w3("S")
+        h_pass(1, 1, 2)
+        h_pass(1, 1, 0)
+        h_pass(1, 2, 0)
+        h_pass(1, 3, 0)
         weave_w1(1, "V")
-        weave_w3("V")
+        h_pass(1, 2, 2)
+        h_pass(1, 1, 1)
+        h_pass(1, 2, 1)
         relu(0, "S")
-        quant_w1()
+        h_pass(1, 3, 1)
         quant_w3()
+        h_pass(1, 0, 3)
+        h_pass(1, 1, 3)
+        h_pass(1, 2, 3)
+        h_pass(1, 3, 3)
+        quant_w1()
+        h_pass(1, 3, 2)
         relu(1, "S")
-        for n in range(2):
-            for c in range(CHUNKS):
-                out_pass(c, n)
-        quant_h(0)
-        relu(2, "S")
         relu(3, "V")
-        for c in range(1, CHUNKS):
-            quant_h(c)
-        for c in range(CHUNKS):
-            out_pass(c, 2)
-        for c in range(CHUNKS):
-            finish(c, "S")
+        out_pass(1, 0)
+        out_pass(3, 0)
+        out_pass(0, 0)
+        out_pass(3, 1)
+        out_pass(0, 1)
+        quant_h(0)
+        out_pass(2, 0)
+        out_pass(2, 1)
+        out_pass(1, 1)
+        quant_h(3)
+        quant_h(1)
+        out_pass(0, 2)
+        out_pass(3, 2)
+        finish(0, "S")
+        out_pass(1, 2)
+        finish(3, "S")
+        finish(1, "S")
+        relu(2, "S")
+        quant_h(2)
+        out_pass(2, 2)
+        finish(2, "S")

@@ -16,311 +16,186 @@ RELU = mybir.ActivationFunctionType.Relu
 MAX = mybir.AluOpType.max
 
 P = 128
-PACK = 4
-K_PASS = P * PACK
+SLOTS = 4
+K_PASS = P * SLOTS
+PASSES = K // K_PASS
+BLOCK = 32
+RUN = BLOCK // SLOTS
+LINE = 4
+SCALE_SHIFT = 4
 CHUNK = 128
 CHUNKS = S // CHUNK
-X_PIECES = ((0, 0, 256), (0, 256, 256), (0, 512, 512), (1, 0, 256), (1, 256, 512), (1, 768, 256))
-TAGS = {"h_codes0":"w3_raw","h_codes1":"w1_raw","w3_bf":"w2_bf1_3"}
-FIRST = ((0, 0, 0, 0), (0, 0, 0, 0))
-W2_PIECES = ((0, 0, 256), (0, 256, 256), (1, 0, 256), (1, 256, 256))
+
+X_PIECES = (
+    (0, 0, 512, 128),
+    (0, 512, 256, 112),
+    (0, 768, 256, 208),
+    (1, 0, 256, 192),
+    (1, 256, 256, 256),
+    (1, 512, 256, 144),
+    (1, 768, 256, 176),
+)
+OFFS_AFTER = 1
+W2_HALF = H // 2
+W2_ON_VECTOR = {(0, 0): 1, (1, 1): 3}
+RELU_ON_VECTOR = (1, 2)
+RESULT_ON_VECTOR = (2, 3)
+WARM_UP = (512, 512)
 
 
 def tile_picked_lora_relu_e_kernel(tc, xT, w1, w2, w3, offs, out):
     nc = tc.nc
     with ExitStack() as ctx:
-        keep = ctx.enter_context(tc.tile_pool(name="keep", bufs=1))
+        sbuf = ctx.enter_context(tc.tile_pool(name="sbuf", bufs=1))
         psum = ctx.enter_context(tc.psum_pool(name="psum", bufs=1))
 
-        made = {}
+        def new_tile(name, shape, dtype, tag=None):
+            return sbuf.tile(shape, dtype, name=name, tag=tag or name, align_bytes=64)
 
-        def sb(name, shape=None, dtype=None):
-            if name not in made:
-                made[name] = keep.tile(shape, dtype, name=name, tag=TAGS.get(name, name), align_bytes=64)
-            return made[name]
-
-        offsets = keep.tile([P, S // 16], U16, name="offsets")
-        x_planes = sb("x_planes", [P, T], U8)
-        nc.gpsimd.memset(x_planes[:].bitcast(U32), 0)
-
-        x_raw = {}
-        w2_raw = {}
-        w1_raw = sb("w1_raw", [P, 2, PACK, N], F32)
-        w3_raw = sb("w3_raw", [P, PACK, N], F32)
-
-        def load_x(n):
-            z, c0, width = X_PIECES[n]
-            x_raw[n] = sb("x_raw%d" % n, [P, PACK, width], F32)
-            rows = xT[z * K_PASS : (z + 1) * K_PASS, c0 : c0 + width]
-            nc.sync.dma_start(out=x_raw[n][:], in_=rows.rearrange("(p j) w -> p j w", j=PACK))
-
-        def load_w2(n):
-            z, c0, width = W2_PIECES[n]
-            w2_raw[n] = sb("w2_raw%d" % n, [P, PACK, width], F32)
-            rows = w2[z * K_PASS : (z + 1) * K_PASS, c0 : c0 + width]
-            nc.sync.dma_start(out=w2_raw[n][:], in_=rows.rearrange("(p j) w -> p j w", j=PACK))
-
-        def load_offs():
-            nc.sync.dma_start(offsets[:], offs)
-
-        def load_w1():
-            nc.sync.dma_start(out=w1_raw[:], in_=w1.rearrange("(z p j) n -> p z j n", z=2, j=PACK))
-
-        def load_w3(t):
-            w3_rows = w3.rearrange("(g t r) n -> t g r n", t=PACK, r=8)
-            nc.sync.dma_start(out=w3_raw[:, t, :], in_=w3_rows[t])
-
-        def weave(engine, dst, src):
-            dst = dst.rearrange("p (c i) j -> p c j i", i=4)
-            src = src.rearrange("p j (c i) -> p c j i", i=4)
-            if engine == "S":
+        def weave(on_scalar, dst, src):
+            dst = dst.rearrange("p (c e) j -> p c j e", e=LINE)
+            src = src.rearrange("p j (c e) -> p c j e", e=LINE)
+            if on_scalar:
                 nc.scalar.activation(dst, src, COPY)
             else:
                 nc.vector.tensor_copy(dst, src)
 
-        def quantize(codes, scales, values):
-            nc.vector.quantize_mx(out=codes.bitcast(FP8X4), scales=scales, in_=values)
+        def quantize(codes, scales, woven):
+            nc.vector.quantize_mx(out=codes.bitcast(FP8X4), scales=scales, in_=woven.rearrange("p c j -> p (c j)"))
 
-        x_codes = [sb("x_codes%d" % z, [P, T], U32) for z in range(2)]
-        x_bf = [sb("x_bf%d" % n, [P, X_PIECES[n][2], PACK], BF16) for n in range(len(X_PIECES))]
+        def matmul(acc, lhs, lhs_scales, rhs, rhs_scales, start, stop):
+            nc.tensor.matmul_mx(
+                out=acc,
+                lhsT=lhs.bitcast(FP8X4),
+                lhsT_scale=lhs_scales,
+                rhs=rhs.bitcast(FP8X4),
+                rhs_scale=rhs_scales,
+                start=start,
+                stop=stop,
+            )
 
-        def weave_x(n, engine, a, b):
-            weave(engine, x_bf[n][:, a:b, :], x_raw[n][:, :, a:b])
+        def chunk_columns(c):
+            return slice(c * CHUNK, (c + 1) * CHUNK)
 
-        def quant_x(n):
-            z, c0, width = X_PIECES[n]
-            quantize(x_codes[z][:, c0 : c0 + width], x_planes[4 * z :, c0 : c0 + width], x_bf[n][:].rearrange("p w j -> p (w j)"))
+        x_scales = new_tile("x_scales", [P, T], U8)
+        nc.gpsimd.memset(x_scales[:].bitcast(U32), 0)
 
-        def pick_codes(z, a, b):
-            nc.vector.tensor_copy(sb("pc%d_%d" % (z, a), [P, (b - a) * CHUNK], U32)[:], x_codes[z][:].indirect(offsets[:, 8 * a : 8 * b]))
+        offsets = sbuf.tile([P, S // 16], U16, name="offsets")
+        x_raw = []
+        for n, (z, first, tokens, share) in enumerate(X_PIECES):
+            x_raw.append(new_tile("x_raw%d" % n, [P, SLOTS, tokens], F32))
+            rows = xT[z * K_PASS : (z + 1) * K_PASS, first : first + tokens]
+            nc.sync.dma_start(out=x_raw[n][:], in_=rows.rearrange("(p j) c -> p j c", j=SLOTS))
+            if n == OFFS_AFTER:
+                nc.sync.dma_start(offsets[:], offs)
+        w2_raw = {}
+        for z in range(PASSES):
+            for half in range(2):
+                w2_raw[z, half] = new_tile("w2_raw%d%d" % (z, half), [P, SLOTS, W2_HALF], F32)
+                rows = w2[z * K_PASS : (z + 1) * K_PASS, half * W2_HALF : (half + 1) * W2_HALF]
+                nc.sync.dma_start(out=w2_raw[z, half][:], in_=rows.rearrange("(p j) c -> p j c", j=SLOTS))
+        w1_raw = new_tile("w1_raw", [P, PASSES, SLOTS, N], F32)
+        nc.sync.dma_start(out=w1_raw[:], in_=w1.rearrange("(z p j) c -> p z j c", z=PASSES, j=SLOTS))
+        w3_raw = new_tile("w3_raw", [P, SLOTS, N], F32)
+        w3_rows = w3.rearrange("(g j r) c -> j g r c", j=SLOTS, r=RUN)
+        for j in range(SLOTS):
+            nc.sync.dma_start(out=w3_raw[:, j, :], in_=w3_rows[j])
 
-        def pick_scales(z, a, b):
-            nc.vector.tensor_copy(sb("ps%d_%d" % (z, a), [P, (b - a) * CHUNK], U8)[:], x_planes[:].indirect(offsets[:, 8 * a : 8 * b]))
+        x_codes = [new_tile("x_codes%d" % z, [P, T], U32) for z in range(PASSES)]
+        picked_codes = [new_tile("picked_codes%d" % z, [P, S], U32) for z in range(PASSES)]
+        picked_scales = new_tile("picked_scales", [P, S], U8)
+        for n, (z, first, tokens, share) in enumerate(X_PIECES):
+            woven = new_tile("x_woven%d" % n, [P, tokens, SLOTS], BF16)
+            weave(True, woven[:, :share, :], x_raw[n][:, :, :share])
+            if share < tokens:
+                weave(False, woven[:, share:, :], x_raw[n][:, :, share:])
+            columns = slice(first, first + tokens)
+            quantize(x_codes[z][:, columns], x_scales[SCALE_SHIFT * z :, columns], woven[:])
+            if first + tokens == T:
+                if z == PASSES - 1:
+                    nc.vector.tensor_copy(picked_scales[:], x_scales[:].indirect(offsets[:]))
+                nc.vector.tensor_copy(picked_codes[z][:], x_codes[z][:].indirect(offsets[:]))
 
-        def picked(z, c, width=CHUNK):
-            a = FIRST[z][c]
-            codes = sb("pc%d_%d" % (z, a))[:, (c - a) * CHUNK : (c - a) * CHUNK + width]
-            a = FIRST[1][c]
-            return codes.bitcast(FP8X4), sb("ps1_%d" % a)[4 * z :, (c - a) * CHUNK : (c - a) * CHUNK + width]
+        def picked(z, columns):
+            return picked_codes[z][:, columns], picked_scales[SCALE_SHIFT * z :, columns]
 
-        def probe(name, src):
-            clock = sb(name, [P, 1], BF16)
-            nc.gpsimd.tensor_copy(clock[:], src)
-
-        h_acc = [psum.tile([P, PACK, CHUNK], F32, name="h_acc%d" % c) for c in range(CHUNKS)]
+        h_acc = [psum.tile([P, SLOTS, CHUNK], F32, name="h_acc%d" % c) for c in range(CHUNKS)]
         out_acc = [psum.tile([P, S], F32, name="out_acc%d" % c) for c in range(CHUNKS)]
-        w2_codes = [sb("w2_codes%d" % z, [P, H], U32) for z in range(2)]
-        w2_scales = [sb("w2_scales%d" % z, [P, H], U8) for z in range(2)]
 
-        def weave_w2(n, engine, t, g0=0, g1=None):
-            z, c0, width = W2_PIECES[n]
-            g1 = width // 32 if g1 is None else g1
-            m0 = c0 // PACK
-            src = w2_raw[n][:, :, 32 * g0 : 32 * g1].rearrange("p j (g t a i) -> p t g a j i", t=PACK, a=2, i=4)
-            dst = sb("w2_bf%d_%d" % (z, t), [P, P, PACK], BF16)[:, m0 + 8 * g0 : m0 + 8 * g1, :].rearrange("p (g a i) j -> p g a j i", a=2, i=4)
-            if engine == "S":
-                nc.scalar.copy(dst, src[:, t])
+        for width in WARM_UP:
+            matmul(out_acc[-1][:, :width], *picked(0, slice(0, P)), *picked(0, slice(0, width)), True, True)
+
+        w2_woven = {}
+        w2_codes = [new_tile("w2_codes%d" % z, [P, H], U32) for z in range(PASSES)]
+        w2_scales = [new_tile("w2_scales%d" % z, [P, H], U8) for z in range(PASSES)]
+
+        def weave_w2(z, half):
+            src = w2_raw[z, half][:].rearrange("p s (g j a e) -> p j g a s e", j=SLOTS, a=RUN // LINE, e=LINE)
+            for j in range(SLOTS):
+                if half == 0:
+                    w2_woven[z, j] = new_tile("w2_woven%d%d" % (z, j), [P, P, SLOTS], BF16)
+                dst = w2_woven[z, j][:, half * P // 2 : (half + 1) * P // 2, :]
+                dst = dst.rearrange("p (g a e) s -> p g a s e", a=RUN // LINE, e=LINE)
+                if j < W2_ON_VECTOR.get((z, half), 0):
+                    nc.vector.tensor_copy(dst, src[:, j])
+                else:
+                    nc.scalar.copy(dst, src[:, j])
+
+        def quantize_w2(z, j):
+            columns = slice(j * P, (j + 1) * P)
+            quantize(w2_codes[z][:, columns], w2_scales[z][:, columns], w2_woven[z, j][:])
+
+        def h_pass(z, j, c):
+            columns = slice(j * P, (j + 1) * P)
+            first, last = (z, j) == (0, 0), (z, j) == (PASSES - 1, SLOTS - 1)
+            matmul(h_acc[c][:, j, :], w2_codes[z][:, columns], w2_scales[z][:, columns], *picked(z, chunk_columns(c)), first, last)
+
+        weave_w2(0, 0)
+        weave_w2(0, 1)
+        for j in range(SLOTS):
+            quantize_w2(0, j)
+            for c in range(CHUNKS):
+                h_pass(0, j, c)
+        weave_w2(1, 0)
+        weave_w2(1, 1)
+        for j in range(SLOTS):
+            quantize_w2(1, j)
+        for c in range(CHUNKS):
+            for j in range(SLOTS):
+                h_pass(1, j, c)
+
+        w1_woven = new_tile("w1_woven", [P, PASSES * N, SLOTS], BF16)
+        w1_codes = new_tile("w1_codes", [P, PASSES * N], U32)
+        w1_scales = new_tile("w1_scales", [P, PASSES * N], U8)
+        w3_woven = new_tile("w3_woven", [P, N, SLOTS], BF16)
+        w3_codes = new_tile("w3_codes", [P, N], U32)
+        w3_scales = new_tile("w3_scales", [P, N], U8)
+        weave(False, w1_woven[:, :N, :], w1_raw[:, 0])
+        weave(True, w1_woven[:, N:, :], w1_raw[:, 1])
+        weave(True, w3_woven[:], w3_raw[:])
+        quantize(w1_codes[:], w1_scales[:], w1_woven[:])
+        quantize(w3_codes[:], w3_scales[:], w3_woven[:])
+        for c in range(CHUNKS):
+            for z in range(PASSES):
+                columns = slice(z * N, (z + 1) * N)
+                matmul(out_acc[c][:, :CHUNK], w1_codes[:, columns], w1_scales[:, columns], *picked(z, chunk_columns(c)), z == 0, False)
+
+        h_woven = new_tile("h_woven", [P, S, SLOTS], BF16, tag="w3_raw")
+        h_codes = new_tile("h_codes", [P, S], U32)
+        h_scales = new_tile("h_scales", [P, S], U8, tag="w1_woven")
+        for c in range(CHUNKS):
+            sums = h_acc[c][:].rearrange("p j c -> p c j")
+            if c in RELU_ON_VECTOR:
+                nc.vector.tensor_scalar(h_woven[:, chunk_columns(c), :], sums, 0.0, None, MAX)
             else:
-                nc.vector.tensor_copy(dst, src[:, t])
-
-        def quant_w2(z, t0=0, t1=PACK):
-            quantize(w2_codes[z][:, t0 * P : t1 * P], w2_scales[z][:, t0 * P : t1 * P], sb("w2_bf%d_%d" % (z, t0))[:].rearrange("p w j -> p (w j)"))
-
-        def h_pass(z, t, c):
-            cols = slice(c * CHUNK, (c + 1) * CHUNK)
-            nc.tensor.matmul_mx(
-                out=h_acc[c][:, t, :],
-                lhsT=w2_codes[z][:, t * P : (t + 1) * P].bitcast(FP8X4),
-                lhsT_scale=w2_scales[z][:, t * P : (t + 1) * P],
-                rhs=picked(z, c)[0],
-                rhs_scale=picked(z, c)[1],
-                start=(z == 0 and t == 0),
-                stop=(z == 1 and t == PACK - 1),
-            )
-
-        def warm(z, width):
-            nc.tensor.matmul_mx(
-                out=out_acc[CHUNKS - 1][:, :width],
-                lhsT=picked(0, 0)[0],
-                lhsT_scale=picked(0, 0)[1],
-                rhs=picked(z, 0, width)[0],
-                rhs_scale=picked(0, 0, width)[1],
-                start=True,
-                stop=True,
-            )
-
-        w1_codes = sb("w1_codes", [P, 2 * N], U32)
-        w1_scales = sb("w1_scales", [P, 2 * N], U8)
-        w3_codes = sb("w3_codes", [P, N], U32)
-        w3_scales = sb("w3_scales", [P, N], U8)
-        h_scales = [sb("h_scales%d" % c, [P, CHUNK], U8) for c in range(CHUNKS)]
-
-        def weave_w1(z, engine):
-            weave(engine, sb("w1_bf", [P, 2, N, PACK], BF16)[:, z], w1_raw[:, z])
-
-        def weave_w3(engine):
-            weave(engine, sb("w3_bf", [P, N, PACK], BF16)[:], w3_raw[:])
-
-        def quant_w1():
-            quantize(w1_codes[:], w1_scales[:], sb("w1_bf")[:].rearrange("p z w j -> p (z w j)"))
-
-        def quant_w3():
-            quantize(w3_codes[:], w3_scales[:], sb("w3_bf")[:].rearrange("p w j -> p (w j)"))
-
-        def relu(c, engine):
-            src = h_acc[c][:].rearrange("p t n -> p n t")
-            dst = sb("h_bf%d" % c, [P, CHUNK, PACK], BF16)
-            if engine == "S":
-                nc.scalar.activation(dst[:], src, RELU)
-            else:
-                nc.vector.tensor_scalar(dst[:], src, 0.0, None, MAX)
-
-        def quant_h(c):
-            quantize(sb("h_codes%d" % c, [P, CHUNK], U32)[:], h_scales[c][:], sb("h_bf%d" % c)[:].rearrange("p w j -> p (w j)"))
-
-        def out_pass(c, n):
-            cols = slice(c * CHUNK, (c + 1) * CHUNK)
-            if n < 2:
-                lhs, lhs_scale = w1_codes[:, n * N : (n + 1) * N], w1_scales[:, n * N : (n + 1) * N]
-                rhs, rhs_scale = picked(n, c)
-            else:
-                lhs, lhs_scale = w3_codes[:], w3_scales[:]
-                rhs, rhs_scale = sb("h_codes%d" % c)[:].bitcast(FP8X4), h_scales[c][:]
-            nc.tensor.matmul_mx(
-                out=out_acc[c][:, :CHUNK], lhsT=lhs.bitcast(FP8X4), lhsT_scale=lhs_scale,
-                rhs=rhs, rhs_scale=rhs_scale, start=(n == 0), stop=(n == 2),
-            )
-
-        def finish(c, engine):
-            result = sb("result%d" % c, [P, CHUNK], F32)
-            if engine == "S":
-                nc.scalar.copy(result[:], out_acc[c][:, :CHUNK])
-            else:
+                nc.scalar.activation(h_woven[:, chunk_columns(c), :], sums, RELU)
+        for c in range(CHUNKS):
+            columns = chunk_columns(c)
+            quantize(h_codes[:, columns], h_scales[:, columns], h_woven[:, columns, :])
+            matmul(out_acc[c][:, :CHUNK], w3_codes[:], w3_scales[:], h_codes[:, columns], h_scales[:, columns], False, True)
+            result = new_tile("result%d" % c, [P, CHUNK], F32)
+            if c in RESULT_ON_VECTOR:
                 nc.vector.tensor_copy(result[:], out_acc[c][:, :CHUNK])
-            nc.sync.dma_start(out=out[:, c * CHUNK : (c + 1) * CHUNK], in_=result[:])
-
-        load_x(0)
-        load_offs()
-        load_x(1)
-        load_x(2)
-        load_x(3)
-        load_x(4)
-        load_x(5)
-        load_w2(0)
-        load_w2(1)
-        load_w2(2)
-        load_w3(0)
-        load_w3(1)
-        load_w3(2)
-        load_w3(3)
-        load_w2(3)
-        load_w1()
-        weave_x(0, "S", 0, 256)
-        weave_x(1, "S", 0, 224)
-        quant_x(0)
-        weave_x(1, "V", 224, 256)
-        quant_x(1)
-        weave_x(2, "S", 0, 160)
-        weave_x(2, "V", 160, 512)
-        weave_x(3, "S", 0, 208)
-        weave_x(3, "V", 208, 256)
-        quant_x(2)
-        pick_codes(0, 0, 4)
-        weave_x(4, "S", 0, 224)
-        quant_x(3)
-        weave_x(4, "V", 224, 512)
-        weave_x(5, "S", 0, 208)
-        weave_w2(0, "S", 0, 0, 6)
-        weave_x(5, "V", 208, 256)
-        quant_x(4)
-        weave_w2(0, "S", 2, 0, 8)
-        quant_x(5)
-        weave_w2(0, "V", 0, 6, 8)
-        weave_w2(0, "S", 3, 0, 8)
-        pick_scales(1, 0, 4)
-        weave_w2(0, "S", 1, 0, 8)
-        weave_w2(1, "S", 1, 0, 8)
-        weave_w2(2, "S", 3, 0, 8)
-        weave_w2(1, "S", 0, 0, 8)
-        weave_w2(1, "S", 3, 0, 8)
-        pick_codes(1, 0, 4)
-        weave_w2(1, "S", 2, 0, 8)
-        weave_w2(2, "S", 1, 0, 8)
-        warm(0, 512)
-        warm(0, 512)
-        quant_w2(0, 3, 4)
-        weave_w2(2, "S", 0, 0, 8)
-        quant_w2(0, 1, 2)
-        warm(0, 256)
-        quant_w2(0, 0, 1)
-        h_pass(0, 0, 1)
-        weave_w2(2, "S", 2, 0, 8)
-        quant_w2(0, 2, 3)
-        h_pass(0, 0, 0)
-        h_pass(0, 0, 3)
-        h_pass(0, 0, 2)
-        h_pass(0, 1, 3)
-        weave_w2(3, "S", 3, 0, 8)
-        weave_w2(3, "V", 0, 0, 8)
-        h_pass(0, 1, 0)
-        h_pass(0, 1, 2)
-        h_pass(0, 1, 1)
-        weave_w2(3, "V", 1, 0, 8)
-        h_pass(0, 2, 3)
-        weave_w2(3, "S", 2, 0, 8)
-        h_pass(0, 2, 0)
-        h_pass(0, 2, 2)
-        quant_w2(1, 0, 1)
-        h_pass(0, 3, 0)
-        h_pass(0, 3, 3)
-        quant_w2(1, 1, 2)
-        h_pass(0, 3, 2)
-        h_pass(0, 2, 1)
-        h_pass(0, 3, 1)
-        quant_w2(1, 3, 4)
-        h_pass(1, 0, 1)
-        quant_w2(1, 2, 3)
-        h_pass(1, 0, 0)
-        h_pass(1, 0, 2)
-        weave_w1(0, "V")
-        weave_w3("S")
-        h_pass(1, 1, 2)
-        h_pass(1, 1, 0)
-        h_pass(1, 2, 0)
-        h_pass(1, 3, 0)
-        weave_w1(1, "V")
-        h_pass(1, 2, 2)
-        h_pass(1, 1, 1)
-        h_pass(1, 2, 1)
-        relu(0, "S")
-        h_pass(1, 3, 1)
-        quant_w3()
-        h_pass(1, 0, 3)
-        h_pass(1, 1, 3)
-        h_pass(1, 2, 3)
-        h_pass(1, 3, 3)
-        quant_w1()
-        h_pass(1, 3, 2)
-        relu(1, "S")
-        relu(3, "V")
-        out_pass(1, 0)
-        out_pass(3, 0)
-        out_pass(0, 0)
-        out_pass(3, 1)
-        out_pass(0, 1)
-        quant_h(0)
-        out_pass(2, 0)
-        out_pass(2, 1)
-        out_pass(1, 1)
-        quant_h(3)
-        quant_h(1)
-        out_pass(0, 2)
-        out_pass(3, 2)
-        finish(0, "S")
-        out_pass(1, 2)
-        finish(3, "S")
-        finish(1, "S")
-        relu(2, "S")
-        quant_h(2)
-        out_pass(2, 2)
-        finish(2, "S")
+            else:
+                nc.scalar.copy(result[:], out_acc[c][:, :CHUNK])
+            nc.sync.dma_start(out=out[:, columns], in_=result[:])

@@ -27,19 +27,19 @@ CHUNK = 128
 CHUNKS = S // CHUNK
 
 X_PIECES = (
-    (0, 0, 512, 128),
-    (0, 512, 256, 112),
-    (0, 768, 256, 208),
-    (1, 0, 256, 192),
-    (1, 256, 256, 256),
-    (1, 512, 256, 144),
-    (1, 768, 256, 176),
+    (0, 0, 512, 224),
+    (0, 512, 256, 160),
+    (0, 768, 256, 112),
+    (1, 0, 256, 224),
+    (1, 256, 256, 208),
+    (1, 512, 256, 176),
+    (1, 768, 256, 160),
 )
 OFFS_AFTER = 1
 W2_HALF = H // 2
 W2_ON_VECTOR = {(0, 0): 1, (1, 1): 3}
-RELU_ON_VECTOR = (1, 2)
-RESULT_ON_VECTOR = (2, 3)
+RELU_ON_VECTOR = (2,)
+RESULT_ON_VECTOR = (1, 2, 3)
 WARM_UP = (512, 512)
 
 
@@ -172,7 +172,7 @@ def tile_picked_lora_relu_e_kernel(tc, xT, w1, w2, w3, offs, out):
         w3_scales = new_tile("w3_scales", [P, N], U8)
         weave(False, w1_woven[:, :N, :], w1_raw[:, 0])
         weave(True, w1_woven[:, N:, :], w1_raw[:, 1])
-        weave(True, w3_woven[:], w3_raw[:])
+        weave(False, w3_woven[:], w3_raw[:])
         quantize(w1_codes[:], w1_scales[:], w1_woven[:])
         quantize(w3_codes[:], w3_scales[:], w3_woven[:])
         for c in range(CHUNKS):
@@ -180,9 +180,9 @@ def tile_picked_lora_relu_e_kernel(tc, xT, w1, w2, w3, offs, out):
                 columns = slice(z * N, (z + 1) * N)
                 matmul(out_acc[c][:, :CHUNK], w1_codes[:, columns], w1_scales[:, columns], *picked(z, chunk_columns(c)), z == 0, False)
 
-        h_woven = new_tile("h_woven", [P, S, SLOTS], BF16, tag="w3_raw")
+        h_woven = new_tile("h_woven", [P, S, SLOTS], BF16)
         h_codes = new_tile("h_codes", [P, S], U32)
-        h_scales = new_tile("h_scales", [P, S], U8, tag="w1_woven")
+        h_scales = new_tile("h_scales", [P, S], U8, tag="w3_raw")
         for c in range(CHUNKS):
             sums = h_acc[c][:].rearrange("p j c -> p c j")
             if c in RELU_ON_VECTOR:

@@ -22,25 +22,24 @@ PASSES = K // K_PASS
 BLOCK = 32
 RUN = BLOCK // SLOTS
 LINE = 4
+LIST_ROWS = 16
 SCALE_SHIFT = 4
 CHUNK = 128
 CHUNKS = S // CHUNK
 
 X_PIECES = (
-    (0, 0, 512, 224),
+    (0, 0, 512, 160),
     (0, 512, 256, 160),
-    (0, 768, 256, 112),
-    (1, 0, 256, 224),
-    (1, 256, 256, 208),
-    (1, 512, 256, 176),
+    (0, 768, 256, 128),
+    (1, 0, 512, 320),
+    (1, 512, 256, 112),
     (1, 768, 256, 160),
 )
-OFFS_AFTER = 1
+OFFS_AFTER = 2
 W2_HALF = H // 2
-W2_ON_VECTOR = {(0, 0): 1, (1, 1): 3}
-RELU_ON_VECTOR = (2,)
-RESULT_ON_VECTOR = (1, 2, 3)
-WARM_UP = (512, 512)
+W2_ON_VECTOR = {(0, 0): 1, (1, 1): 2}
+RELU_ON_VECTOR = 0
+RESULT_ON_VECTOR = (2, 3)
 
 
 def tile_picked_lora_relu_e_kernel(tc, xT, w1, w2, w3, offs, out):
@@ -53,15 +52,15 @@ def tile_picked_lora_relu_e_kernel(tc, xT, w1, w2, w3, offs, out):
             return sbuf.tile(shape, dtype, name=name, tag=tag or name, align_bytes=64)
 
         def weave(on_scalar, dst, src):
-            dst = dst.rearrange("p (c e) j -> p c j e", e=LINE)
-            src = src.rearrange("p j (c e) -> p c j e", e=LINE)
+            dst = dst.rearrange("p (a b) j -> p a j b", b=LINE)
+            src = src.rearrange("p j (a b) -> p a j b", b=LINE)
             if on_scalar:
                 nc.scalar.activation(dst, src, COPY)
             else:
                 nc.vector.tensor_copy(dst, src)
 
         def quantize(codes, scales, woven):
-            nc.vector.quantize_mx(out=codes.bitcast(FP8X4), scales=scales, in_=woven.rearrange("p c j -> p (c j)"))
+            nc.vector.quantize_mx(out=codes.bitcast(FP8X4), scales=scales, in_=woven.rearrange("p w j -> p (w j)"))
 
         def matmul(acc, lhs, lhs_scales, rhs, rhs_scales, start, stop):
             nc.tensor.matmul_mx(
@@ -80,62 +79,67 @@ def tile_picked_lora_relu_e_kernel(tc, xT, w1, w2, w3, offs, out):
         x_scales = new_tile("x_scales", [P, T], U8)
         nc.gpsimd.memset(x_scales[:].bitcast(U32), 0)
 
-        offsets = sbuf.tile([P, S // 16], U16, name="offsets")
+        offsets = sbuf.tile([P, S // LIST_ROWS], U16, name="offsets")
         x_raw = []
-        for n, (z, first, tokens, share) in enumerate(X_PIECES):
-            x_raw.append(new_tile("x_raw%d" % n, [P, SLOTS, tokens], F32))
-            rows = xT[z * K_PASS : (z + 1) * K_PASS, first : first + tokens]
-            nc.sync.dma_start(out=x_raw[n][:], in_=rows.rearrange("(p j) c -> p j c", j=SLOTS))
-            if n == OFFS_AFTER:
+        for piece in range(len(X_PIECES)):
+            z, first_token, tokens = X_PIECES[piece][:3]
+            x_raw.append(new_tile("x_raw%d" % piece, [P, SLOTS, tokens], F32))
+            rows = xT[z * K_PASS : (z + 1) * K_PASS, first_token : first_token + tokens]
+            nc.sync.dma_start(out=x_raw[piece][:], in_=rows.rearrange("(p j) w -> p j w", j=SLOTS))
+            if piece == OFFS_AFTER:
                 nc.sync.dma_start(offsets[:], offs)
         w2_raw = {}
         for z in range(PASSES):
             for half in range(2):
                 w2_raw[z, half] = new_tile("w2_raw%d%d" % (z, half), [P, SLOTS, W2_HALF], F32)
                 rows = w2[z * K_PASS : (z + 1) * K_PASS, half * W2_HALF : (half + 1) * W2_HALF]
-                nc.sync.dma_start(out=w2_raw[z, half][:], in_=rows.rearrange("(p j) c -> p j c", j=SLOTS))
+                nc.sync.dma_start(out=w2_raw[z, half][:], in_=rows.rearrange("(p j) w -> p j w", j=SLOTS))
         w1_raw = new_tile("w1_raw", [P, PASSES, SLOTS, N], F32)
-        nc.sync.dma_start(out=w1_raw[:], in_=w1.rearrange("(z p j) c -> p z j c", z=PASSES, j=SLOTS))
+        nc.sync.dma_start(out=w1_raw[:], in_=w1.rearrange("(z p j) w -> p z j w", z=PASSES, j=SLOTS))
         w3_raw = new_tile("w3_raw", [P, SLOTS, N], F32)
-        w3_rows = w3.rearrange("(g j r) c -> j g r c", j=SLOTS, r=RUN)
+        w3_rows = w3.rearrange("(g j r) w -> j g r w", j=SLOTS, r=RUN)
         for j in range(SLOTS):
             nc.sync.dma_start(out=w3_raw[:, j, :], in_=w3_rows[j])
 
         x_codes = [new_tile("x_codes%d" % z, [P, T], U32) for z in range(PASSES)]
-        picked_codes = [new_tile("picked_codes%d" % z, [P, S], U32) for z in range(PASSES)]
+        picked_codes = {}
         picked_scales = new_tile("picked_scales", [P, S], U8)
-        for n, (z, first, tokens, share) in enumerate(X_PIECES):
-            woven = new_tile("x_woven%d" % n, [P, tokens, SLOTS], BF16)
-            weave(True, woven[:, :share, :], x_raw[n][:, :, :share])
-            if share < tokens:
-                weave(False, woven[:, share:, :], x_raw[n][:, :, share:])
-            columns = slice(first, first + tokens)
-            quantize(x_codes[z][:, columns], x_scales[SCALE_SHIFT * z :, columns], woven[:])
-            if first + tokens == T:
-                if z == PASSES - 1:
-                    nc.vector.tensor_copy(picked_scales[:], x_scales[:].indirect(offsets[:]))
-                nc.vector.tensor_copy(picked_codes[z][:], x_codes[z][:].indirect(offsets[:]))
 
-        def picked(z, columns):
-            return picked_codes[z][:, columns], picked_scales[SCALE_SHIFT * z :, columns]
+        def pick_codes(z, chunks, tag=None):
+            gathered = new_tile("picked_codes%d%d" % (z, chunks.start), [P, len(chunks) * CHUNK], U32, tag)
+            entries = offsets[:, chunks.start * CHUNK // LIST_ROWS : chunks.stop * CHUNK // LIST_ROWS]
+            nc.vector.tensor_copy(gathered[:], x_codes[z][:].indirect(entries))
+            for c in chunks:
+                picked_codes[z, c] = gathered[:, chunk_columns(c - chunks.start)]
+
+        for piece, (z, first_token, tokens, share) in enumerate(X_PIECES):
+            x_woven = new_tile("x_woven%d" % piece, [P, tokens, SLOTS], BF16)
+            weave(True, x_woven[:, :share, :], x_raw[piece][:, :, :share])
+            weave(False, x_woven[:, share:, :], x_raw[piece][:, :, share:])
+            columns = slice(first_token, first_token + tokens)
+            quantize(x_codes[z][:, columns], x_scales[SCALE_SHIFT * z :, columns], x_woven[:])
+            if (z, columns.stop) == (0, T):
+                pick_codes(0, range(CHUNKS))
+        nc.vector.tensor_copy(picked_scales[:], x_scales[:].indirect(offsets[:]))
+        pick_codes(1, range(CHUNKS // 2))
+
+        def picked(z, c):
+            return picked_codes[z, c], picked_scales[SCALE_SHIFT * z :, chunk_columns(c)]
 
         h_acc = [psum.tile([P, SLOTS, CHUNK], F32, name="h_acc%d" % c) for c in range(CHUNKS)]
-        out_acc = [psum.tile([P, S], F32, name="out_acc%d" % c) for c in range(CHUNKS)]
-
-        for width in WARM_UP:
-            matmul(out_acc[-1][:, :width], *picked(0, slice(0, P)), *picked(0, slice(0, width)), True, True)
+        out_acc = [psum.tile([P, CHUNK], F32, name="out_acc%d" % c) for c in range(CHUNKS)]
 
         w2_woven = {}
         w2_codes = [new_tile("w2_codes%d" % z, [P, H], U32) for z in range(PASSES)]
         w2_scales = [new_tile("w2_scales%d" % z, [P, H], U8) for z in range(PASSES)]
 
         def weave_w2(z, half):
-            src = w2_raw[z, half][:].rearrange("p s (g j a e) -> p j g a s e", j=SLOTS, a=RUN // LINE, e=LINE)
+            src = w2_raw[z, half][:].rearrange("p s (g j a b) -> p j g a s b", j=SLOTS, a=RUN // LINE, b=LINE)
             for j in range(SLOTS):
                 if half == 0:
                     w2_woven[z, j] = new_tile("w2_woven%d%d" % (z, j), [P, P, SLOTS], BF16)
                 dst = w2_woven[z, j][:, half * P // 2 : (half + 1) * P // 2, :]
-                dst = dst.rearrange("p (g a e) s -> p g a s e", a=RUN // LINE, e=LINE)
+                dst = dst.rearrange("p (g a b) s -> p g a s b", a=RUN // LINE, b=LINE)
                 if j < W2_ON_VECTOR.get((z, half), 0):
                     nc.vector.tensor_copy(dst, src[:, j])
                 else:
@@ -147,8 +151,8 @@ def tile_picked_lora_relu_e_kernel(tc, xT, w1, w2, w3, offs, out):
 
         def h_pass(z, j, c):
             columns = slice(j * P, (j + 1) * P)
-            first, last = (z, j) == (0, 0), (z, j) == (PASSES - 1, SLOTS - 1)
-            matmul(h_acc[c][:, j, :], w2_codes[z][:, columns], w2_scales[z][:, columns], *picked(z, chunk_columns(c)), first, last)
+            start, stop = (z, j) == (0, 0), (z, j) == (PASSES - 1, SLOTS - 1)
+            matmul(h_acc[c][:, j, :], w2_codes[z][:, columns], w2_scales[z][:, columns], *picked(z, c), start, stop)
 
         weave_w2(0, 0)
         weave_w2(0, 1)
@@ -156,6 +160,7 @@ def tile_picked_lora_relu_e_kernel(tc, xT, w1, w2, w3, offs, out):
             quantize_w2(0, j)
             for c in range(CHUNKS):
                 h_pass(0, j, c)
+        pick_codes(1, range(CHUNKS // 2, CHUNKS), tag="w2_woven01")
         weave_w2(1, 0)
         weave_w2(1, 1)
         for j in range(SLOTS):
@@ -178,24 +183,26 @@ def tile_picked_lora_relu_e_kernel(tc, xT, w1, w2, w3, offs, out):
         for c in range(CHUNKS):
             for z in range(PASSES):
                 columns = slice(z * N, (z + 1) * N)
-                matmul(out_acc[c][:, :CHUNK], w1_codes[:, columns], w1_scales[:, columns], *picked(z, chunk_columns(c)), z == 0, False)
+                matmul(out_acc[c][:], w1_codes[:, columns], w1_scales[:, columns], *picked(z, c), z == 0, False)
 
-        h_woven = new_tile("h_woven", [P, S, SLOTS], BF16)
+        h_woven = []
         h_codes = new_tile("h_codes", [P, S], U32)
         h_scales = new_tile("h_scales", [P, S], U8, tag="w3_raw")
         for c in range(CHUNKS):
-            sums = h_acc[c][:].rearrange("p j c -> p c j")
-            if c in RELU_ON_VECTOR:
-                nc.vector.tensor_scalar(h_woven[:, chunk_columns(c), :], sums, 0.0, None, MAX)
+            sums = h_acc[c][:].rearrange("p j w -> p w j")
+            if c == RELU_ON_VECTOR:
+                h_woven.append(new_tile("h_woven%d" % c, [P, CHUNK, SLOTS], BF16, tag="w1_raw"))
+                nc.vector.tensor_scalar(h_woven[c][:], sums, 0.0, None, MAX)
             else:
-                nc.scalar.activation(h_woven[:, chunk_columns(c), :], sums, RELU)
+                h_woven.append(new_tile("h_woven%d" % c, [P, CHUNK, SLOTS], BF16))
+                nc.scalar.activation(h_woven[c][:], sums, RELU)
         for c in range(CHUNKS):
             columns = chunk_columns(c)
-            quantize(h_codes[:, columns], h_scales[:, columns], h_woven[:, columns, :])
-            matmul(out_acc[c][:, :CHUNK], w3_codes[:], w3_scales[:], h_codes[:, columns], h_scales[:, columns], False, True)
+            quantize(h_codes[:, columns], h_scales[:, columns], h_woven[c][:])
+            matmul(out_acc[c][:], w3_codes[:], w3_scales[:], h_codes[:, columns], h_scales[:, columns], False, True)
             result = new_tile("result%d" % c, [P, CHUNK], F32)
             if c in RESULT_ON_VECTOR:
-                nc.vector.tensor_copy(result[:], out_acc[c][:, :CHUNK])
+                nc.vector.tensor_copy(result[:], out_acc[c][:])
             else:
-                nc.scalar.copy(result[:], out_acc[c][:, :CHUNK])
+                nc.scalar.copy(result[:], out_acc[c][:])
             nc.sync.dma_start(out=out[:, columns], in_=result[:])

from contextlib import ExitStack

import concourse.mybir as mybir

K, T, S, H, N = 1024, 1024, 512, 512, 128
FLOPS = 2 * S * (K * N + K * H + H * N)

F32 = mybir.dt.float32
BF16 = mybir.dt.bfloat16
U32 = mybir.dt.uint32
U16 = mybir.dt.uint16
U8 = mybir.dt.uint8
FP8X4 = mybir.dt.float8_e4m3fn_x4
COPY = mybir.ActivationFunctionType.Copy
RELU = mybir.ActivationFunctionType.Relu
MAX = mybir.AluOpType.max

P = 128
SLOTS = 4
K_PASS = P * SLOTS
PASSES = K // K_PASS
BLOCK = 32
RUN = BLOCK // SLOTS
LINE = 4
LIST_ROWS = 16
SCALE_SHIFT = 4
CHUNK = 128
CHUNKS = S // CHUNK

X_PIECES = (
    (0, 0, 512, 160),
    (0, 512, 256, 160),
    (0, 768, 256, 128),
    (1, 0, 512, 320),
    (1, 512, 256, 112),
    (1, 768, 256, 160),
)
OFFS_AFTER = 2
W2_HALF = H // 2
W2_ON_VECTOR = {(0, 0): 1, (1, 1): 2}
RELU_ON_VECTOR = 0
RESULT_ON_VECTOR = (2, 3)


def tile_picked_lora_relu_e_kernel(tc, xT, w1, w2, w3, offs, out):
    nc = tc.nc
    with ExitStack() as ctx:
        sbuf = ctx.enter_context(tc.tile_pool(name="sbuf", bufs=1))
        psum = ctx.enter_context(tc.psum_pool(name="psum", bufs=1))

        def new_tile(name, shape, dtype, tag=None):
            return sbuf.tile(shape, dtype, name=name, tag=tag or name, align_bytes=64)

        def weave(on_scalar, dst, src):
            dst = dst.rearrange("p (a b) j -> p a j b", b=LINE)
            src = src.rearrange("p j (a b) -> p a j b", b=LINE)
            if on_scalar:
                nc.scalar.activation(dst, src, COPY)
            else:
                nc.vector.tensor_copy(dst, src)

        def quantize(codes, scales, woven):
            nc.vector.quantize_mx(out=codes.bitcast(FP8X4), scales=scales, in_=woven.rearrange("p w j -> p (w j)"))

        def matmul(acc, lhs, lhs_scales, rhs, rhs_scales, start, stop):
            nc.tensor.matmul_mx(
                out=acc,
                lhsT=lhs.bitcast(FP8X4),
                lhsT_scale=lhs_scales,
                rhs=rhs.bitcast(FP8X4),
                rhs_scale=rhs_scales,
                start=start,
                stop=stop,
            )

        def chunk_columns(c):
            return slice(c * CHUNK, (c + 1) * CHUNK)

        x_scales = new_tile("x_scales", [P, T], U8)
        nc.gpsimd.memset(x_scales[:].bitcast(U32), 0)

        offsets = sbuf.tile([P, S // LIST_ROWS], U16, name="offsets")
        x_raw = []
        for piece in range(len(X_PIECES)):
            z, first_token, tokens = X_PIECES[piece][:3]
            x_raw.append(new_tile("x_raw%d" % piece, [P, SLOTS, tokens], F32))
            rows = xT[z * K_PASS : (z + 1) * K_PASS, first_token : first_token + tokens]
            nc.sync.dma_start(out=x_raw[piece][:], in_=rows.rearrange("(p j) w -> p j w", j=SLOTS))
            if piece == OFFS_AFTER:
                nc.sync.dma_start(offsets[:], offs)
        w2_raw = {}
        for z in range(PASSES):
            for half in range(2):
                w2_raw[z, half] = new_tile("w2_raw%d%d" % (z, half), [P, SLOTS, W2_HALF], F32)
                rows = w2[z * K_PASS : (z + 1) * K_PASS, half * W2_HALF : (half + 1) * W2_HALF]
                nc.sync.dma_start(out=w2_raw[z, half][:], in_=rows.rearrange("(p j) w -> p j w", j=SLOTS))
        w1_raw = new_tile("w1_raw", [P, PASSES, SLOTS, N], F32)
        nc.sync.dma_start(out=w1_raw[:], in_=w1.rearrange("(z p j) w -> p z j w", z=PASSES, j=SLOTS))
        w3_raw = new_tile("w3_raw", [P, SLOTS, N], F32)
        w3_rows = w3.rearrange("(g j r) w -> j g r w", j=SLOTS, r=RUN)
        for j in range(SLOTS):
            nc.sync.dma_start(out=w3_raw[:, j, :], in_=w3_rows[j])

        x_codes = [new_tile("x_codes%d" % z, [P, T], U32) for z in range(PASSES)]
        picked_codes = {}
        picked_scales = new_tile("picked_scales", [P, S], U8)

        def pick_codes(z, chunks, tag=None):
            gathered = new_tile("picked_codes%d%d" % (z, chunks.start), [P, len(chunks) * CHUNK], U32, tag)
            entries = offsets[:, chunks.start * CHUNK // LIST_ROWS : chunks.stop * CHUNK // LIST_ROWS]
            nc.vector.tensor_copy(gathered[:], x_codes[z][:].indirect(entries))
            for c in chunks:
                picked_codes[z, c] = gathered[:, chunk_columns(c - chunks.start)]

        for piece, (z, first_token, tokens, share) in enumerate(X_PIECES):
            x_woven = new_tile("x_woven%d" % piece, [P, tokens, SLOTS], BF16)
            weave(True, x_woven[:, :share, :], x_raw[piece][:, :, :share])
            weave(False, x_woven[:, share:, :], x_raw[piece][:, :, share:])
            columns = slice(first_token, first_token + tokens)
            quantize(x_codes[z][:, columns], x_scales[SCALE_SHIFT * z :, columns], x_woven[:])
            if (z, columns.stop) == (0, T):
                pick_codes(0, range(CHUNKS))
        nc.vector.tensor_copy(picked_scales[:], x_scales[:].indirect(offsets[:]))
        pick_codes(1, range(CHUNKS // 2))

        def picked(z, c):
            return picked_codes[z, c], picked_scales[SCALE_SHIFT * z :, chunk_columns(c)]

        h_acc = [psum.tile([P, SLOTS, CHUNK], F32, name="h_acc%d" % c) for c in range(CHUNKS)]
        out_acc = [psum.tile([P, CHUNK], F32, name="out_acc%d" % c) for c in range(CHUNKS)]

        w2_woven = {}
        w2_codes = [new_tile("w2_codes%d" % z, [P, H], U32) for z in range(PASSES)]
        w2_scales = [new_tile("w2_scales%d" % z, [P, H], U8) for z in range(PASSES)]

        def weave_w2(z, half):
            src = w2_raw[z, half][:].rearrange("p s (g j a b) -> p j g a s b", j=SLOTS, a=RUN // LINE, b=LINE)
            for j in range(SLOTS):
                if half == 0:
                    w2_woven[z, j] = new_tile("w2_woven%d%d" % (z, j), [P, P, SLOTS], BF16)
                dst = w2_woven[z, j][:, half * P // 2 : (half + 1) * P // 2, :]
                dst = dst.rearrange("p (g a b) s -> p g a s b", a=RUN // LINE, b=LINE)
                if j < W2_ON_VECTOR.get((z, half), 0):
                    nc.vector.tensor_copy(dst, src[:, j])
                else:
                    nc.scalar.copy(dst, src[:, j])

        def quantize_w2(z, j):
            columns = slice(j * P, (j + 1) * P)
            quantize(w2_codes[z][:, columns], w2_scales[z][:, columns], w2_woven[z, j][:])

        def h_pass(z, j, c):
            columns = slice(j * P, (j + 1) * P)
            start, stop = (z, j) == (0, 0), (z, j) == (PASSES - 1, SLOTS - 1)
            matmul(h_acc[c][:, j, :], w2_codes[z][:, columns], w2_scales[z][:, columns], *picked(z, c), start, stop)

        weave_w2(0, 0)
        weave_w2(0, 1)
        for j in range(SLOTS):
            quantize_w2(0, j)
            for c in range(CHUNKS):
                h_pass(0, j, c)
        pick_codes(1, range(CHUNKS // 2, CHUNKS), tag="w2_woven01")
        weave_w2(1, 0)
        weave_w2(1, 1)
        for j in range(SLOTS):
            quantize_w2(1, j)
        for c in range(CHUNKS):
            for j in range(SLOTS):
                h_pass(1, j, c)

        w1_woven = new_tile("w1_woven", [P, PASSES * N, SLOTS], BF16)
        w1_codes = new_tile("w1_codes", [P, PASSES * N], U32)
        w1_scales = new_tile("w1_scales", [P, PASSES * N], U8)
        w3_woven = new_tile("w3_woven", [P, N, SLOTS], BF16)
        w3_codes = new_tile("w3_codes", [P, N], U32)
        w3_scales = new_tile("w3_scales", [P, N], U8)
        weave(False, w1_woven[:, :N, :], w1_raw[:, 0])
        weave(True, w1_woven[:, N:, :], w1_raw[:, 1])
        weave(False, w3_woven[:], w3_raw[:])
        quantize(w1_codes[:], w1_scales[:], w1_woven[:])
        quantize(w3_codes[:], w3_scales[:], w3_woven[:])
        for c in range(CHUNKS):
            for z in range(PASSES):
                columns = slice(z * N, (z + 1) * N)
                matmul(out_acc[c][:], w1_codes[:, columns], w1_scales[:, columns], *picked(z, c), z == 0, False)

        h_woven = []
        h_codes = new_tile("h_codes", [P, S], U32)
        h_scales = new_tile("h_scales", [P, S], U8, tag="w3_raw")
        for c in range(CHUNKS):
            sums = h_acc[c][:].rearrange("p j w -> p w j")
            if c == RELU_ON_VECTOR:
                h_woven.append(new_tile("h_woven%d" % c, [P, CHUNK, SLOTS], BF16, tag="w1_raw"))
                nc.vector.tensor_scalar(h_woven[c][:], sums, 0.0, None, MAX)
            else:
                h_woven.append(new_tile("h_woven%d" % c, [P, CHUNK, SLOTS], BF16))
                nc.scalar.activation(h_woven[c][:], sums, RELU)
        for c in range(CHUNKS):
            columns = chunk_columns(c)
            quantize(h_codes[:, columns], h_scales[:, columns], h_woven[c][:])
            matmul(out_acc[c][:], w3_codes[:], w3_scales[:], h_codes[:, columns], h_scales[:, columns], False, True)
            result = new_tile("result%d" % c, [P, CHUNK], F32)
            if c in RESULT_ON_VECTOR:
                nc.vector.tensor_copy(result[:], out_acc[c][:])
            else:
                nc.scalar.copy(result[:], out_acc[c][:])
            nc.sync.dma_start(out=out[:, columns], in_=result[:])
